import numpy as np
import ml_dtypes


def mxq(x, axis, fmt="e4m3"):
    dtype, down = {"e4m3": (ml_dtypes.float8_e4m3fn, 7), "e5m2": (ml_dtypes.float8_e5m2, 14)}[fmt]
    v = np.moveaxis(np.asarray(x, np.float32).astype(ml_dtypes.bfloat16).astype(np.float64), axis, -1)
    blocks = v.reshape(v.shape[:-1] + (-1, 32))
    amax = np.abs(blocks).max(-1, keepdims=True)
    byte = np.maximum(np.where(amax > 0, np.frexp(amax)[1] - 1 + 127, 0) - down, 1)
    scale = np.exp2(byte - 127.0)
    codes = (blocks / scale).astype(np.float32).astype(dtype).astype(np.float64)
    return np.moveaxis((codes * scale).reshape(v.shape), -1, axis)


WIDE = False


def mx_kscale(k, group=512):
    if not WIDE:
        return np.ones(k)
    levels = np.array([18, -18])
    if group != 512:
        return np.exp2(np.random.permutation(np.resize(levels, k // group))).repeat(group)
    if k % 512:
        return np.exp2(np.random.permutation(np.resize(levels, k // 32))).repeat(32)
    a = np.empty((k // 512, 16))
    for p in range(k // 512):
        a[p, :8] = np.random.permutation(np.resize(levels, 8))
        for g in range(8):
            far = levels[np.abs(levels - a[p, g]) >= 10]
            a[p, g + 8] = far[np.random.randint(len(far))]
    return np.exp2(a.ravel()).repeat(32)


def f64(x):
    return np.asarray(x).astype(np.float64)


def silu(v):
    return v / (1.0 + np.exp(-v))


G, D, M, N = 4, 128, 128, 1024


def setup_inputs():
    n = np.random.standard_normal
    s = mx_kscale(D, 0)[:, None]
    return {
        "x": (n((G, D, N)) * s).astype(np.float32),
        "w": (n((G, D, M)) / np.sqrt(D) / s).astype(np.float32),
        "b": (0.5 * n((G, M, 1))).astype(np.float32),
        "r": n((G, M, N)).astype(np.float32),
    }


def reference(x, w, b, r):
    xq = mxq(f64(x), 1, "e4m3")
    y = mxq(f64(w), 1, "e4m3").transpose(0, 2, 1) @ xq
    y = y + f64(b)
    y = silu(y)
    y = y + f64(r)
    return y

@@ -1,0 +1,127 @@
+from contextlib import ExitStack
+
+import concourse.mybir as mybir
+
+G, D, M, N = 4, 128, 128, 1024
+FLOPS = 2 * G * D * M * N
+
+F32 = mybir.dt.float32
+BF16 = mybir.dt.bfloat16
+U32 = mybir.dt.uint32
+U8 = mybir.dt.uint8
+FP8X4 = mybir.dt.float8_e4m3fn_x4
+SILU = mybir.ActivationFunctionType.Silu
+
+P = 128
+PACK = 4
+ROWS = D // PACK
+HALF = 512
+RUN = 4
+VECTOR_COLS = 344
+
+
+def interleave(copy, packed, raw, c0, c1):
+    copy(
+        out=packed[:, c0:c1, :].rearrange("p (c i) t -> p c t i", i=RUN),
+        in_=raw[:, :, c0:c1].rearrange("p t (c i) -> p c t i", i=RUN),
+    )
+
+
+def quantise(nc, codes, scales, packed):
+    nc.vector.quantize_mx(
+        out=codes[:].bitcast(FP8X4),
+        scales=scales[:],
+        in_=packed[:].rearrange("p c t -> p (c t)"),
+    )
+
+
+def tile_rows_glin_silu_bias_res_kernel(tc, x, w, b, r, out):
+    nc = tc.nc
+    x_rows = x.rearrange("g (p t) n -> (g p) t n", t=PACK)
+    w_rows = w.rearrange("g (p t) m -> (g p) t m", t=PACK)
+
+    with ExitStack() as ctx:
+        sb = ctx.enter_context(tc.tile_pool(name="sb", bufs=1))
+        ps = ctx.enter_context(tc.psum_pool(name="ps", bufs=1))
+        ctx.enter_context(tc.manual_schedule())
+
+        bias_rows = sb.tile([P, M], F32, name="bias_rows", align_bytes=64)
+        bias_cols = sb.tile([P, M], F32, name="bias_cols", align_bytes=64)
+        w_raw = sb.tile([P, PACK, M], F32, name="w_raw", align_bytes=64)
+        w_packed = sb.tile([P, M, PACK], BF16, name="w_packed", align_bytes=64)
+        w_codes = sb.tile([P, M], U32, name="w_codes", align_bytes=64)
+        w_scales = sb.tile([P, M], U8, name="w_scales", align_bytes=64)
+        x_raw, x_packed, x_codes, x_scales = [], [], [], []
+        for h in range(2):
+            x_raw.append(sb.tile([P, PACK, HALF], F32, name="x_raw%d" % h, align_bytes=64))
+            x_packed.append(sb.tile([P, HALF, PACK], BF16, name="x_packed%d" % h, align_bytes=64))
+            x_codes.append(sb.tile([P, HALF], U32, name="x_codes%d" % h, align_bytes=64))
+            x_scales.append(sb.tile([P, HALF], U8, name="x_scales%d" % h, align_bytes=64))
+        res, act, result, acc = [], [], [], []
+        for g in range(G):
+            res.append(sb.tile([P, N], F32, name="res%d" % g, align_bytes=64))
+            act.append(sb.tile([P, N], F32, name="act%d" % g, align_bytes=64))
+            result.append(sb.tile([P, N], F32, name="result%d" % g, align_bytes=64))
+            acc.append([ps.tile([P, HALF], F32, name="acc%d_%d" % (g, h)) for h in range(2)])
+
+        def cols(h):
+            return slice(h * HALF, (h + 1) * HALF)
+
+        def multiply(h):
+            for g in range(G):
+                rows = slice(ROWS * g, ROWS * (g + 1))
+                nc.tensor.matmul_mx(
+                    out=acc[g][h][:],
+                    lhsT=w_codes[rows, :].bitcast(FP8X4),
+                    lhsT_scale=w_scales[rows, :],
+                    rhs=x_codes[h][rows, :].bitcast(FP8X4),
+                    rhs_scale=x_scales[h][rows, :],
+                    start=True,
+                    stop=True,
+                )
+
+        def activate(g, h):
+            nc.scalar.activation(
+                out=act[g][:, cols(h)], in_=acc[g][h][:], func=SILU, bias=bias_cols[:, ROWS * g : ROWS * g + 1]
+            )
+
+        def add_residual(g, h):
+            nc.vector.tensor_add(out=result[g][:, cols(h)], in0=act[g][:, cols(h)], in1=res[g][:, cols(h)])
+
+        nc.vector.memset(bias_rows[:], 0.0)
+        nc.sync.dma_start(out=w_raw[:], in_=w_rows)
+        nc.sync.dma_start(out=x_raw[0][:], in_=x_rows[:, :, cols(0)])
+        nc.sync.dma_start(
+            out=bias_rows[0:P:ROWS, :].rearrange("c (g i) -> c g i", g=G),
+            in_=b.rearrange("g (c i) o -> c g (i o)", c=G),
+        )
+        nc.sync.dma_start(out=x_raw[1][:], in_=x_rows[:, :, cols(1)])
+        for g in range(G):
+            nc.sync.dma_start(out=res[g][:], in_=r[g])
+
+        interleave(nc.vector.tensor_copy, w_packed, w_raw, 0, M)
+        quantise(nc, w_codes, w_scales, w_packed)
+
+        interleave(nc.vector.tensor_copy, x_packed[0], x_raw[0], 0, HALF)
+        nc.vector.transpose(out=bias_cols[:], in_=bias_rows[:])
+        quantise(nc, x_codes[0], x_scales[0], x_packed[0])
+        multiply(0)
+        activate(0, 0)
+        activate(1, 0)
+
+        interleave(nc.vector.tensor_copy, x_packed[1], x_raw[1], 0, VECTOR_COLS)
+        interleave(nc.scalar.copy, x_packed[1], x_raw[1], VECTOR_COLS, HALF)
+        quantise(nc, x_codes[1], x_scales[1], x_packed[1])
+        multiply(1)
+        activate(2, 0)
+        activate(3, 0)
+        for g in range(G):
+            activate(g, 1)
+
+        add_residual(0, 0)
+        add_residual(1, 0)
+        for g in range(G):
+            if g >= 2:
+                add_residual(g, 0)
+            add_residual(g, 1)
+            nc.sync.dma_start(out=out[g], in_=result[g][:])

@@ -118,10 +118,9 @@ def tile_rows_glin_silu_bias_res_kernel(tc, x, w, b, r, out):
         for g in range(G):
             activate(g, 1)
 
-        add_residual(0, 0)
-        add_residual(1, 0)
-        for g in range(G):
-            if g >= 2:
-                add_residual(g, 0)
-            add_residual(g, 1)
-            nc.sync.dma_start(out=out[g], in_=result[g][:])
+        for g, h in ((0, 0), (1, 0), (0, 1), (1, 1), (2, 0), (2, 1), (3, 0), (3, 1)):
+            add_residual(g, h)
+            if g != 2:
+                nc.sync.dma_start(out=out[g, :, cols(h)], in_=result[g][:, cols(h)])
+            elif h == 1:
+                nc.sync.dma_start(out=out[g], in_=result[g][:])

@@ -17,21 +17,23 @@ PACK = 4
 ROWS = D // PACK
 HALF = 512
 RUN = 4
-VECTOR_COLS = 344
+FIRST = 640
+SPLIT_FIRST = 432
+SPLIT_SECOND = 896
 
 
-def interleave(copy, packed, raw, c0, c1):
+def interleave(copy, packed, raw):
     copy(
-        out=packed[:, c0:c1, :].rearrange("p (c i) t -> p c t i", i=RUN),
-        in_=raw[:, :, c0:c1].rearrange("p t (c i) -> p c t i", i=RUN),
+        out=packed.rearrange("p (c i) t -> p c t i", i=RUN),
+        in_=raw.rearrange("p t (c i) -> p c t i", i=RUN),
     )
 
 
-def quantise(nc, codes, scales, packed):
+def quantise(nc, codes, scales, packed, c0, c1):
     nc.vector.quantize_mx(
-        out=codes[:].bitcast(FP8X4),
-        scales=scales[:],
-        in_=packed[:].rearrange("p c t -> p (c t)"),
+        out=codes[:, c0:c1].bitcast(FP8X4),
+        scales=scales[:, c0:c1],
+        in_=packed[:, c0:c1, :].rearrange("p c t -> p (c t)"),
     )
 
 
@@ -51,12 +53,11 @@ def tile_rows_glin_silu_bias_res_kernel(tc, x, w, b, r, out):
         w_packed = sb.tile([P, M, PACK], BF16, name="w_packed", align_bytes=64)
         w_codes = sb.tile([P, M], U32, name="w_codes", align_bytes=64)
         w_scales = sb.tile([P, M], U8, name="w_scales", align_bytes=64)
-        x_raw, x_packed, x_codes, x_scales = [], [], [], []
-        for h in range(2):
-            x_raw.append(sb.tile([P, PACK, HALF], F32, name="x_raw%d" % h, align_bytes=64))
-            x_packed.append(sb.tile([P, HALF, PACK], BF16, name="x_packed%d" % h, align_bytes=64))
-            x_codes.append(sb.tile([P, HALF], U32, name="x_codes%d" % h, align_bytes=64))
-            x_scales.append(sb.tile([P, HALF], U8, name="x_scales%d" % h, align_bytes=64))
+        x_first = sb.tile([P, PACK, FIRST], F32, name="x_first", align_bytes=64)
+        x_second = sb.tile([P, PACK, N - FIRST], F32, name="x_second", align_bytes=64)
+        x_packed = sb.tile([P, N, PACK], BF16, name="x_packed", align_bytes=64)
+        x_codes = sb.tile([P, N], U32, name="x_codes", align_bytes=64)
+        x_scales = sb.tile([P, N], U8, name="x_scales", align_bytes=64)
         res, act, result, acc = [], [], [], []
         for g in range(G):
             res.append(sb.tile([P, N], F32, name="res%d" % g, align_bytes=64))
@@ -67,18 +68,17 @@ def tile_rows_glin_silu_bias_res_kernel(tc, x, w, b, r, out):
         def cols(h):
             return slice(h * HALF, (h + 1) * HALF)
 
-        def multiply(h):
-            for g in range(G):
-                rows = slice(ROWS * g, ROWS * (g + 1))
-                nc.tensor.matmul_mx(
-                    out=acc[g][h][:],
-                    lhsT=w_codes[rows, :].bitcast(FP8X4),
-                    lhsT_scale=w_scales[rows, :],
-                    rhs=x_codes[h][rows, :].bitcast(FP8X4),
-                    rhs_scale=x_scales[h][rows, :],
-                    start=True,
-                    stop=True,
-                )
+        def multiply(g, h):
+            rows = slice(ROWS * g, ROWS * (g + 1))
+            nc.tensor.matmul_mx(
+                out=acc[g][h][:],
+                lhsT=w_codes[rows, :].bitcast(FP8X4),
+                lhsT_scale=w_scales[rows, :],
+                rhs=x_codes[rows, cols(h)].bitcast(FP8X4),
+                rhs_scale=x_scales[rows, cols(h)],
+                start=True,
+                stop=True,
+            )
 
         def activate(g, h):
             nc.scalar.activation(
@@ -88,39 +88,44 @@ def tile_rows_glin_silu_bias_res_kernel(tc, x, w, b, r, out):
         def add_residual(g, h):
             nc.vector.tensor_add(out=result[g][:, cols(h)], in0=act[g][:, cols(h)], in1=res[g][:, cols(h)])
 
+        warm = sb.tile([P, 1], F32, name="warm")
+        warm_in = sb.tile([P, 1], F32, name="warm_in")
         nc.vector.memset(bias_rows[:], 0.0)
+        nc.vector.memset(warm_in[:], 0.0)
+        nc.scalar.activation(out=warm[:], in_=warm_in[:], func=SILU)
+        nc.sync.dma_start(out=x_first[:], in_=x_rows[:, :, 0:FIRST])
         nc.sync.dma_start(out=w_raw[:], in_=w_rows)
-        nc.sync.dma_start(out=x_raw[0][:], in_=x_rows[:, :, cols(0)])
         nc.sync.dma_start(
             out=bias_rows[0:P:ROWS, :].rearrange("c (g i) -> c g i", g=G),
             in_=b.rearrange("g (c i) o -> c g (i o)", c=G),
         )
-        nc.sync.dma_start(out=x_raw[1][:], in_=x_rows[:, :, cols(1)])
+        nc.sync.dma_start(out=x_second[:], in_=x_rows[:, :, FIRST:N])
         for g in range(G):
-            nc.sync.dma_start(out=res[g][:], in_=r[g])
+            if g == 2:
+                for h in range(2):
+                    nc.sync.dma_start(out=res[g][:, cols(h)], in_=r[g, :, cols(h)])
+            else:
+                nc.sync.dma_start(out=res[g][:], in_=r[g])
 
-        interleave(nc.vector.tensor_copy, w_packed, w_raw, 0, M)
-        quantise(nc, w_codes, w_scales, w_packed)
-
-        interleave(nc.vector.tensor_copy, x_packed[0], x_raw[0], 0, HALF)
+        interleave(nc.vector.tensor_copy, x_packed[:, 0:SPLIT_FIRST, :], x_first[:, :, 0:SPLIT_FIRST])
+        interleave(nc.scalar.copy, x_packed[:, SPLIT_FIRST:FIRST, :], x_first[:, :, SPLIT_FIRST:FIRST])
+        interleave(nc.scalar.copy, w_packed[:], w_raw[:])
         nc.vector.transpose(out=bias_cols[:], in_=bias_rows[:])
-        quantise(nc, x_codes[0], x_scales[0], x_packed[0])
-        multiply(0)
-        activate(0, 0)
-        activate(1, 0)
+        quantise(nc, x_codes, x_scales, x_packed, 0, HALF)
+        quantise(nc, x_codes, x_scales, x_packed, HALF, FIRST)
+        quantise(nc, w_codes, w_scales, w_packed, 0, M)
+        order = ((0, 0), (1, 0), (2, 0), (0, 1), (1, 1), (2, 1), (3, 0), (3, 1))
+        for g, h in order[:3]:
+            multiply(g, h)
 
-        interleave(nc.vector.tensor_copy, x_packed[1], x_raw[1], 0, VECTOR_COLS)
-        interleave(nc.scalar.copy, x_packed[1], x_raw[1], VECTOR_COLS, HALF)
-        quantise(nc, x_codes[1], x_scales[1], x_packed[1])
-        multiply(1)
-        activate(2, 0)
-        activate(3, 0)
-        for g in range(G):
-            activate(g, 1)
-
-        for g, h in ((0, 0), (1, 0), (0, 1), (1, 1), (2, 0), (2, 1), (3, 0), (3, 1)):
+        interleave(nc.vector.tensor_copy, x_packed[:, FIRST:SPLIT_SECOND, :], x_second[:, :, 0 : SPLIT_SECOND - FIRST])
+        interleave(nc.scalar.copy, x_packed[:, SPLIT_SECOND:N, :], x_second[:, :, SPLIT_SECOND - FIRST : N - FIRST])
+        quantise(nc, x_codes, x_scales, x_packed, SPLIT_SECOND, N)
+        quantise(nc, x_codes, x_scales, x_packed, FIRST, SPLIT_SECOND)
+        for g, h in order[3:]:
+            multiply(g, h)
+        for g, h in order:
+            activate(g, h)
+        for g, h in order:
             add_residual(g, h)
-            if g != 2:
-                nc.sync.dma_start(out=out[g, :, cols(h)], in_=result[g][:, cols(h)])
-            elif h == 1:
-                nc.sync.dma_start(out=out[g], in_=result[g][:])
+            nc.sync.dma_start(out=out[g, :, cols(h)], in_=result[g][:, cols(h)])

@@ -17,9 +17,9 @@ PACK = 4
 ROWS = D // PACK
 HALF = 512
 RUN = 4
-FIRST = 640
-SPLIT_FIRST = 432
-SPLIT_SECOND = 896
+QUARTER = 256
+SPLIT_FIRST = 344
+EIGHTH = 128
 
 
 def interleave(copy, packed, raw):
@@ -42,6 +42,9 @@ def tile_rows_glin_silu_bias_res_kernel(tc, x, w, b, r, out):
     x_rows = x.rearrange("g (p t) n -> (g p) t n", t=PACK)
     w_rows = w.rearrange("g (p t) m -> (g p) t m", t=PACK)
 
+    r_rows = r.rearrange("g m n -> m g n")
+    out_rows = out.rearrange("g m n -> m g n")
+
     with ExitStack() as ctx:
         sb = ctx.enter_context(tc.tile_pool(name="sb", bufs=1))
         ps = ctx.enter_context(tc.psum_pool(name="ps", bufs=1))
@@ -53,17 +56,19 @@ def tile_rows_glin_silu_bias_res_kernel(tc, x, w, b, r, out):
         w_packed = sb.tile([P, M, PACK], BF16, name="w_packed", align_bytes=64)
         w_codes = sb.tile([P, M], U32, name="w_codes", align_bytes=64)
         w_scales = sb.tile([P, M], U8, name="w_scales", align_bytes=64)
-        x_first = sb.tile([P, PACK, FIRST], F32, name="x_first", align_bytes=64)
-        x_second = sb.tile([P, PACK, N - FIRST], F32, name="x_second", align_bytes=64)
+        bounds = (0, HALF, HALF + QUARTER, N)
+        x_raw = []
+        for k in range(3):
+            x_raw.append(sb.tile([P, PACK, bounds[k + 1] - bounds[k]], F32, name="x_raw%d" % k, align_bytes=64))
         x_packed = sb.tile([P, N, PACK], BF16, name="x_packed", align_bytes=64)
         x_codes = sb.tile([P, N], U32, name="x_codes", align_bytes=64)
         x_scales = sb.tile([P, N], U8, name="x_scales", align_bytes=64)
         res, act, result, acc = [], [], [], []
-        for g in range(G):
-            res.append(sb.tile([P, N], F32, name="res%d" % g, align_bytes=64))
-            act.append(sb.tile([P, N], F32, name="act%d" % g, align_bytes=64))
-            result.append(sb.tile([P, N], F32, name="result%d" % g, align_bytes=64))
-            acc.append([ps.tile([P, HALF], F32, name="acc%d_%d" % (g, h)) for h in range(2)])
+        for h in range(2):
+            res.append([sb.tile([P, 2, HALF], F32, name="res%d_%d" % (h, k), align_bytes=64) for k in range(2)])
+            act.append(sb.tile([P, G, HALF], F32, name="act%d" % h, align_bytes=64))
+            result.append(sb.tile([P, G, HALF], F32, name="result%d" % h, align_bytes=64))
+            acc.append([ps.tile([P, HALF], F32, name="acc%d_%d" % (h, g)) for g in range(G)])
 
         def cols(h):
             return slice(h * HALF, (h + 1) * HALF)
@@ -71,7 +76,7 @@ def tile_rows_glin_silu_bias_res_kernel(tc, x, w, b, r, out):
         def multiply(g, h):
             rows = slice(ROWS * g, ROWS * (g + 1))
             nc.tensor.matmul_mx(
-                out=acc[g][h][:],
+                out=acc[h][g][:],
                 lhsT=w_codes[rows, :].bitcast(FP8X4),
                 lhsT_scale=w_scales[rows, :],
                 rhs=x_codes[rows, cols(h)].bitcast(FP8X4),
@@ -82,50 +87,62 @@ def tile_rows_glin_silu_bias_res_kernel(tc, x, w, b, r, out):
 
         def activate(g, h):
             nc.scalar.activation(
-                out=act[g][:, cols(h)], in_=acc[g][h][:], func=SILU, bias=bias_cols[:, ROWS * g : ROWS * g + 1]
+                out=act[h][:, g, :], in_=acc[h][g][:], func=SILU, bias=bias_cols[:, ROWS * g : ROWS * g + 1]
             )
 
         def add_residual(g, h):
-            nc.vector.tensor_add(out=result[g][:, cols(h)], in0=act[g][:, cols(h)], in1=res[g][:, cols(h)])
+            nc.vector.tensor_add(out=result[h][:, g, :], in0=act[h][:, g, :], in1=res[h][g // 2][:, g % 2, :])
+
+        def store(g0, g1, h):
+            nc.sync.dma_start(out=out_rows[:, g0:g1, cols(h)], in_=result[h][:, g0:g1, :])
+
+        def pack(copy, k, c0, c1):
+            interleave(copy, x_packed[:, c0:c1, :], x_raw[k][:, :, c0 - bounds[k] : c1 - bounds[k]])
 
         warm = sb.tile([P, 1], F32, name="warm")
         warm_in = sb.tile([P, 1], F32, name="warm_in")
         nc.vector.memset(bias_rows[:], 0.0)
         nc.vector.memset(warm_in[:], 0.0)
         nc.scalar.activation(out=warm[:], in_=warm_in[:], func=SILU)
-        nc.sync.dma_start(out=x_first[:], in_=x_rows[:, :, 0:FIRST])
+        nc.sync.dma_start(out=x_raw[0][:], in_=x_rows[:, :, 0:HALF])
         nc.sync.dma_start(out=w_raw[:], in_=w_rows)
         nc.sync.dma_start(
             out=bias_rows[0:P:ROWS, :].rearrange("c (g i) -> c g i", g=G),
             in_=b.rearrange("g (c i) o -> c g (i o)", c=G),
         )
-        nc.sync.dma_start(out=x_second[:], in_=x_rows[:, :, FIRST:N])
-        for g in range(G):
-            if g == 2:
-                for h in range(2):
-                    nc.sync.dma_start(out=res[g][:, cols(h)], in_=r[g, :, cols(h)])
-            else:
-                nc.sync.dma_start(out=res[g][:], in_=r[g])
+        for k in (1, 2):
+            nc.sync.dma_start(out=x_raw[k][:], in_=x_rows[:, :, bounds[k] : bounds[k + 1]])
+        for h in range(2):
+            for k in range(2):
+                nc.sync.dma_start(out=res[h][k][:], in_=r_rows[:, 2 * k : 2 * k + 2, cols(h)])
 
-        interleave(nc.vector.tensor_copy, x_packed[:, 0:SPLIT_FIRST, :], x_first[:, :, 0:SPLIT_FIRST])
-        interleave(nc.scalar.copy, x_packed[:, SPLIT_FIRST:FIRST, :], x_first[:, :, SPLIT_FIRST:FIRST])
+        pack(nc.vector.tensor_copy, 0, 0, SPLIT_FIRST)
+        pack(nc.scalar.copy, 0, SPLIT_FIRST, HALF)
         interleave(nc.scalar.copy, w_packed[:], w_raw[:])
         nc.vector.transpose(out=bias_cols[:], in_=bias_rows[:])
         quantise(nc, x_codes, x_scales, x_packed, 0, HALF)
-        quantise(nc, x_codes, x_scales, x_packed, HALF, FIRST)
         quantise(nc, w_codes, w_scales, w_packed, 0, M)
-        order = ((0, 0), (1, 0), (2, 0), (0, 1), (1, 1), (2, 1), (3, 0), (3, 1))
-        for g, h in order[:3]:
-            multiply(g, h)
+        for g in range(G):
+            multiply(g, 0)
 
-        interleave(nc.vector.tensor_copy, x_packed[:, FIRST:SPLIT_SECOND, :], x_second[:, :, 0 : SPLIT_SECOND - FIRST])
-        interleave(nc.scalar.copy, x_packed[:, SPLIT_SECOND:N, :], x_second[:, :, SPLIT_SECOND - FIRST : N - FIRST])
-        quantise(nc, x_codes, x_scales, x_packed, SPLIT_SECOND, N)
-        quantise(nc, x_codes, x_scales, x_packed, FIRST, SPLIT_SECOND)
-        for g, h in order[3:]:
-            multiply(g, h)
-        for g, h in order:
-            activate(g, h)
-        for g, h in order:
-            add_residual(g, h)
-            nc.sync.dma_start(out=out[g, :, cols(h)], in_=result[g][:, cols(h)])
+        pack(nc.vector.tensor_copy, 1, bounds[1], bounds[2])
+        quantise(nc, x_codes, x_scales, x_packed, bounds[1], bounds[2])
+        activate(0, 0)
+        for c0 in range(bounds[2], N, EIGHTH):
+            pack(nc.vector.tensor_copy, 2, c0, c0 + EIGHTH)
+        for c0 in range(bounds[2], N, EIGHTH):
+            quantise(nc, x_codes, x_scales, x_packed, c0, c0 + EIGHTH)
+        for g in range(G):
+            multiply(g, 1)
+        for g in range(1, G):
+            activate(g, 0)
+        for g in range(G):
+            activate(g, 1)
+
+        for h in range(2):
+            for g in range(G):
+                add_residual(g, h)
+                if h == 0 and g < 2:
+                    store(g, g + 1, h)
+                elif g % 2 == 1:
+                    store(g - 1, g + 1, h)

@@ -99,11 +99,7 @@ def tile_rows_glin_silu_bias_res_kernel(tc, x, w, b, r, out):
         def pack(copy, k, c0, c1):
             interleave(copy, x_packed[:, c0:c1, :], x_raw[k][:, :, c0 - bounds[k] : c1 - bounds[k]])
 
-        warm = sb.tile([P, 1], F32, name="warm")
-        warm_in = sb.tile([P, 1], F32, name="warm_in")
         nc.vector.memset(bias_rows[:], 0.0)
-        nc.vector.memset(warm_in[:], 0.0)
-        nc.scalar.activation(out=warm[:], in_=warm_in[:], func=SILU)
         nc.sync.dma_start(out=x_raw[0][:], in_=x_rows[:, :, 0:HALF])
         nc.sync.dma_start(out=w_raw[:], in_=w_rows)
         nc.sync.dma_start(

from contextlib import ExitStack

import concourse.mybir as mybir

G, D, M, N = 4, 128, 128, 1024
FLOPS = 2 * G * D * M * N

F32 = mybir.dt.float32
BF16 = mybir.dt.bfloat16
U32 = mybir.dt.uint32
U8 = mybir.dt.uint8
FP8X4 = mybir.dt.float8_e4m3fn_x4
SILU = mybir.ActivationFunctionType.Silu

P = 128
PACK = 4
ROWS = D // PACK
HALF = 512
RUN = 4
QUARTER = 256
SPLIT_FIRST = 344
EIGHTH = 128


def interleave(copy, packed, raw):
    copy(
        out=packed.rearrange("p (c i) t -> p c t i", i=RUN),
        in_=raw.rearrange("p t (c i) -> p c t i", i=RUN),
    )


def quantise(nc, codes, scales, packed, c0, c1):
    nc.vector.quantize_mx(
        out=codes[:, c0:c1].bitcast(FP8X4),
        scales=scales[:, c0:c1],
        in_=packed[:, c0:c1, :].rearrange("p c t -> p (c t)"),
    )


def tile_rows_glin_silu_bias_res_kernel(tc, x, w, b, r, out):
    nc = tc.nc
    x_rows = x.rearrange("g (p t) n -> (g p) t n", t=PACK)
    w_rows = w.rearrange("g (p t) m -> (g p) t m", t=PACK)

    r_rows = r.rearrange("g m n -> m g n")
    out_rows = out.rearrange("g m n -> m g n")

    with ExitStack() as ctx:
        sb = ctx.enter_context(tc.tile_pool(name="sb", bufs=1))
        ps = ctx.enter_context(tc.psum_pool(name="ps", bufs=1))
        ctx.enter_context(tc.manual_schedule())

        bias_rows = sb.tile([P, M], F32, name="bias_rows", align_bytes=64)
        bias_cols = sb.tile([P, M], F32, name="bias_cols", align_bytes=64)
        w_raw = sb.tile([P, PACK, M], F32, name="w_raw", align_bytes=64)
        w_packed = sb.tile([P, M, PACK], BF16, name="w_packed", align_bytes=64)
        w_codes = sb.tile([P, M], U32, name="w_codes", align_bytes=64)
        w_scales = sb.tile([P, M], U8, name="w_scales", align_bytes=64)
        bounds = (0, HALF, HALF + QUARTER, N)
        x_raw = []
        for k in range(3):
            x_raw.append(sb.tile([P, PACK, bounds[k + 1] - bounds[k]], F32, name="x_raw%d" % k, align_bytes=64))
        x_packed = sb.tile([P, N, PACK], BF16, name="x_packed", align_bytes=64)
        x_codes = sb.tile([P, N], U32, name="x_codes", align_bytes=64)
        x_scales = sb.tile([P, N], U8, name="x_scales", align_bytes=64)
        res, act, result, acc = [], [], [], []
        for h in range(2):
            res.append([sb.tile([P, 2, HALF], F32, name="res%d_%d" % (h, k), align_bytes=64) for k in range(2)])
            act.append(sb.tile([P, G, HALF], F32, name="act%d" % h, align_bytes=64))
            result.append(sb.tile([P, G, HALF], F32, name="result%d" % h, align_bytes=64))
            acc.append([ps.tile([P, HALF], F32, name="acc%d_%d" % (h, g)) for g in range(G)])

        def cols(h):
            return slice(h * HALF, (h + 1) * HALF)

        def multiply(g, h):
            rows = slice(ROWS * g, ROWS * (g + 1))
            nc.tensor.matmul_mx(
                out=acc[h][g][:],
                lhsT=w_codes[rows, :].bitcast(FP8X4),
                lhsT_scale=w_scales[rows, :],
                rhs=x_codes[rows, cols(h)].bitcast(FP8X4),
                rhs_scale=x_scales[rows, cols(h)],
                start=True,
                stop=True,
            )

        def activate(g, h):
            nc.scalar.activation(
                out=act[h][:, g, :], in_=acc[h][g][:], func=SILU, bias=bias_cols[:, ROWS * g : ROWS * g + 1]
            )

        def add_residual(g, h):
            nc.vector.tensor_add(out=result[h][:, g, :], in0=act[h][:, g, :], in1=res[h][g // 2][:, g % 2, :])

        def store(g0, g1, h):
            nc.sync.dma_start(out=out_rows[:, g0:g1, cols(h)], in_=result[h][:, g0:g1, :])

        def pack(copy, k, c0, c1):
            interleave(copy, x_packed[:, c0:c1, :], x_raw[k][:, :, c0 - bounds[k] : c1 - bounds[k]])

        nc.vector.memset(bias_rows[:], 0.0)
        nc.sync.dma_start(out=x_raw[0][:], in_=x_rows[:, :, 0:HALF])
        nc.sync.dma_start(out=w_raw[:], in_=w_rows)
        nc.sync.dma_start(
            out=bias_rows[0:P:ROWS, :].rearrange("c (g i) -> c g i", g=G),
            in_=b.rearrange("g (c i) o -> c g (i o)", c=G),
        )
        for k in (1, 2):
            nc.sync.dma_start(out=x_raw[k][:], in_=x_rows[:, :, bounds[k] : bounds[k + 1]])
        for h in range(2):
            for k in range(2):
                nc.sync.dma_start(out=res[h][k][:], in_=r_rows[:, 2 * k : 2 * k + 2, cols(h)])

        pack(nc.vector.tensor_copy, 0, 0, SPLIT_FIRST)
        pack(nc.scalar.copy, 0, SPLIT_FIRST, HALF)
        interleave(nc.scalar.copy, w_packed[:], w_raw[:])
        nc.vector.transpose(out=bias_cols[:], in_=bias_rows[:])
        quantise(nc, x_codes, x_scales, x_packed, 0, HALF)
        quantise(nc, w_codes, w_scales, w_packed, 0, M)
        for g in range(G):
            multiply(g, 0)

        pack(nc.vector.tensor_copy, 1, bounds[1], bounds[2])
        quantise(nc, x_codes, x_scales, x_packed, bounds[1], bounds[2])
        activate(0, 0)
        for c0 in range(bounds[2], N, EIGHTH):
            pack(nc.vector.tensor_copy, 2, c0, c0 + EIGHTH)
        for c0 in range(bounds[2], N, EIGHTH):
            quantise(nc, x_codes, x_scales, x_packed, c0, c0 + EIGHTH)
        for g in range(G):
            multiply(g, 1)
        for g in range(1, G):
            activate(g, 0)
        for g in range(G):
            activate(g, 1)

        for h in range(2):
            for g in range(G):
                add_residual(g, h)
                if h == 0 and g < 2:
                    store(g, g + 1, h)
                elif g % 2 == 1:
                    store(g - 1, g + 1, h)
